import numpy as np
import ml_dtypes


def mxq(x, axis, fmt="e4m3"):
    dtype, down = {"e4m3": (ml_dtypes.float8_e4m3fn, 7), "e5m2": (ml_dtypes.float8_e5m2, 14)}[fmt]
    v = np.moveaxis(np.asarray(x, np.float32).astype(ml_dtypes.bfloat16).astype(np.float64), axis, -1)
    blocks = v.reshape(v.shape[:-1] + (-1, 32))
    amax = np.abs(blocks).max(-1, keepdims=True)
    byte = np.maximum(np.where(amax > 0, np.frexp(amax)[1] - 1 + 127, 0) - down, 1)
    scale = np.exp2(byte - 127.0)
    codes = (blocks / scale).astype(np.float32).astype(dtype).astype(np.float64)
    return np.moveaxis((codes * scale).reshape(v.shape), -1, axis)


WIDE = False


def mx_kscale(k):
    if not WIDE:
        return np.ones(k)
    levels = np.array([10, -10, 5, -5, 0])
    if k % 512:
        return np.exp2(np.random.permutation(np.resize(levels, k // 32))).repeat(32)
    a = np.empty((k // 512, 16))
    for p in range(k // 512):
        a[p, :8] = np.random.permutation(np.resize(levels, 8))
        for g in range(8):
            far = levels[np.abs(levels - a[p, g]) >= 10]
            a[p, g + 8] = far[np.random.randint(len(far))]
    return np.exp2(a.ravel()).repeat(32)


def f64(x):
    return np.asarray(x).astype(np.float64)


def striped(idx):
    return np.tile(idx.reshape(-1, 16).T, (8, 1)).astype(np.uint16)


def unstriped(offs):
    return offs[:16].T.reshape(-1).astype(np.int64)


E2M1 = np.array([0.0, 0.5, 1.0, 1.5, 2.0, 3.0, 4.0, 6.0, -0.0, -0.5, -1.0, -1.5, -2.0, -3.0, -4.0, -6.0])


def pack_weight(w, fmt):
    k, n = w.shape
    w = f64(np.asarray(w, np.float32).astype(ml_dtypes.bfloat16)).reshape(k // 32, 32, n)
    amax = np.abs(w).max(1)
    if fmt == "e4m3":
        byte = np.frexp(amax)[1] - 1 + 127 - 7
    else:
        mant, ex = np.frexp(amax / 6.0)
        byte = np.where(mant > 0.5, ex, ex - 1) + 127
    byte = np.clip(np.where(amax > 0, byte, 1), 1, 254)
    scaled = (w * np.exp2(127.0 - byte)[:, None, :]).reshape(k, n).astype(np.float32)
    by_word = np.ascontiguousarray(scaled.reshape(k // 512, 128, 4, n).transpose(0, 1, 3, 2))
    if fmt == "e4m3":
        words = by_word.astype(ml_dtypes.float8_e4m3fn).view(np.uint8)
    else:
        c = by_word.astype(ml_dtypes.float4_e2m1fn).view(np.uint8) & 0xF
        words = (c[..., 0::2] | (c[..., 1::2] << 4)).reshape(k // 512, 128, 2 * n)
    return np.ascontiguousarray(words), np.ascontiguousarray(byte.astype(np.uint8).reshape(k // 512, 16, n))


def unpack_weight(words, scales, fmt):
    g, _, n = scales.shape
    words = np.ascontiguousarray(words).reshape(g, 128, n, -1)
    if fmt == "e4m3":
        vals = words.view(ml_dtypes.float8_e4m3fn).astype(np.float64)
    else:
        nib = np.empty((g, 128, n, 4), np.uint8)
        nib[..., 0::2] = words & 0xF
        nib[..., 1::2] = words >> 4
        vals = E2M1[nib]
    vals = vals * np.repeat(np.exp2(scales.astype(np.float64) - 127.0), 8, axis=1)[..., None]
    return vals.transpose(0, 1, 3, 2).reshape(g * 512, n)


def gelu(v):
    return 0.5 * v * (1.0 + np.tanh(np.sqrt(2.0 / np.pi) * (v + 0.044715 * v**3)))


K, H, N, T, S, P, T2 = 1536, 1024, 512, 2048, 1024, 1024, 2048


def setup_inputs():
    n = np.random.standard_normal
    s = mx_kscale(K)[:, None]
    u = mx_kscale(H)[:, None]
    d = {}
    d["tab_words"], d["tab_scales"] = pack_weight(n((K, T)) * s, "e4m3")
    d["offs"] = striped(np.random.permutation(T)[:S])
    d["offs2"] = striped(np.random.permutation(T2)[:S])
    d["offs3"] = striped(np.random.permutation(T2)[:P])
    d["offs4"] = striped(np.random.permutation(T2)[:P])
    d["w1_words"], d["w1_scales"] = pack_weight(1.3 * n((K, H)) / s / K ** 0.5, "e2m1")
    d["mix"] = (1.5 * n((H, S))).astype(np.float32)
    d["gain"] = (0.6 * np.exp(0.3 * n(H)) * u[:, 0]).astype(np.float32)
    d["wgs"] = np.exp(0.3 * n((128, S))).astype(np.float32)
    d["page0"] = (n((H, T2)) * u).astype(np.float32)
    d["low"] = ((0.4 * n(H) - 0.4) * u[:, 0]).astype(np.float32)
    d["w4"] = (n((H, N)) / u / H ** 0.5).astype(np.float32)
    d["target"] = (0.8 * n(N)).astype(np.float32)
    d["wgo"] = np.exp(0.3 * n((128, P))).astype(np.float32)
    d["page1"] = n((N, T2)).astype(np.float32)
    return d


def reference(tab_words, tab_scales, offs, offs2, offs3, offs4, w1_words, w1_scales, mix, gain, wgs, page0, low, w4, target, wgo, page1):
    v = unpack_weight(tab_words, tab_scales, "e4m3")[:, unstriped(offs)]
    a = unpack_weight(w1_words, w1_scales, "e2m1").T @ v
    h = (np.tanh(a) * f64(mix) + a) * f64(gain)[:, None]
    page = f64(page0).copy()
    page[:, unstriped(offs2)] = np.tile(f64(wgs), (H // 128, 1)) * h
    x = np.maximum(page[:, unstriped(offs3)], f64(low)[:, None])
    e = mxq(f64(w4), 0, "e4m3").T @ mxq(x, 0, "e4m3")
    y = np.square(e - f64(target)[:, None])
    out = f64(page1).copy()
    out[:, unstriped(offs4)] = np.tile(f64(wgo), (N // 128, 1)) * y
    return out

@@ -1,0 +1,296 @@
+from contextlib import ExitStack
+
+import concourse.mybir as mybir
+from concourse.masks import make_identity
+
+K, H, N, T, S, M, T2 = 1536, 1024, 512, 2048, 1024, 1024, 2048
+FLOPS = 2 * K * H * S + 2 * H * N * M
+
+F32 = mybir.dt.float32
+BF16 = mybir.dt.bfloat16
+I32 = mybir.dt.int32
+U32 = mybir.dt.uint32
+U16 = mybir.dt.uint16
+U8 = mybir.dt.uint8
+FP8X4 = mybir.dt.float8_e4m3fn_x4
+FP4X4 = mybir.dt.float4_e2m1fn_x4
+ACT = mybir.ActivationFunctionType
+ALU = mybir.AluOpType
+
+P = 128
+PACK = 4
+PASS = P * PACK
+HALF = 512
+KP = K // PASS
+HP = H // PASS
+NQ = N // P
+WIDE_BUFS = 8
+
+
+def half_cols(h):
+    return slice(h * HALF, (h + 1) * HALF)
+
+
+def half_offsets(tile, h):
+    return tile[:, h * HALF // 16 : (h + 1) * HALF // 16]
+
+
+def tile_list_overrun_valve_features_kernel(
+    tc, tab_words, tab_scales, offs, offs2, offs3, offs4, w1_words, w1_scales, mix, gain, wgs, page0, low, w4, target, wgo, page1, out
+):
+    nc = tc.nc
+    with ExitStack() as ctx:
+        keep = ctx.enter_context(tc.tile_pool(name="keep", bufs=1))
+        ring = ctx.enter_context(tc.tile_pool(name="ring", bufs=2))
+        psum = ctx.enter_context(tc.psum_pool(name="psum", bufs=2))
+
+        def wide(shape, dtype, name):
+            return ring.tile(shape, dtype, name=name, tag="wide", bufs=WIDE_BUFS)
+
+        lists = [keep.tile([P, S // 16], U16, name="list%d" % i) for i in range(4)]
+        l_tab, l_put, l_get, l_out = lists
+
+        tab_sc = keep.tile([P, T], U8)
+        w1_sc = keep.tile([P, KP, H], U8, align_bytes=64)
+        moved = keep.tile([P, KP - 1, S], U8, align_bytes=64)
+        nc.gpsimd.memset(w1_sc[:].bitcast(I32), 0)
+        nc.vector.memset(tab_sc[:].bitcast(I32), 0)
+        nc.vector.memset(moved[:].bitcast(I32), 0)
+
+        nc.sync.dma_start(l_tab[:], offs)
+        tabs = [wide([P, T], I32, "tab%d" % a) for a in range(KP - 1)]
+        tabs.append(keep.tile([P, T], I32, name="tab2", tag="tablast", align_bytes=64))
+
+        def load_tab(a):
+            nc.sync.dma_start(tabs[a][:], tab_words[a].rearrange("p t i -> p (t i)").bitcast(I32))
+
+        load_tab(0)
+        staged = keep.tile([P, T // 4], I32)
+        for q in range(4):
+            eng = nc.sync if q < 2 else nc.scalar
+            live = slice(32 * q, 32 * q + 4 * KP)
+            eng.dma_start(staged[live, :], tab_scales[:, 4 * q : 4 * q + 4, :].bitcast(I32))
+            nc.vector.tensor_copy(tab_sc[live, :].bitcast(I32), staged[live, :])
+        load_tab(1)
+        load_tab(2)
+        for q in range(4):
+            nc.gpsimd.dma_start(
+                w1_sc[32 * q : 32 * q + 4, :, :].bitcast(I32),
+                w1_scales[:, 4 * q : 4 * q + 4, :].rearrange("a r c -> r a c").bitcast(I32),
+            )
+        ident = keep.tile([P, P], F32)
+        make_identity(nc, ident[:])
+        gain_sb = keep.tile([P, HP, PACK], F32)
+        low_sb = keep.tile([P, HP, PACK], F32)
+        target_sb = keep.tile([P, NQ], F32)
+        nc.gpsimd.dma_start(gain_sb[:], gain.rearrange("(b p t) -> p b t", b=HP, t=PACK))
+        nc.gpsimd.dma_start(low_sb[:], low.rearrange("(b p t) -> p b t", b=HP, t=PACK))
+
+        w1_w = [keep.tile([P, KP, 2 * PASS], U8, name="w1w%d" % b, align_bytes=64) for b in range(HP)]
+
+        def load_w1(b):
+            nc.sync.dma_start(
+                w1_w[b][:].bitcast(I32),
+                w1_words[:, :, 2 * PASS * b : 2 * PASS * (b + 1)].rearrange("a p c -> p a c").bitcast(I32),
+            )
+
+        load_w1(0)
+
+        got_sc = keep.tile([P, S], U8, align_bytes=64)
+        nc.vector.tensor_copy(got_sc[:], tab_sc[:].indirect(l_tab[:]))
+        for a in range(1, KP):
+            nc.scalar.dma_start(moved[0:112, a - 1, :].bitcast(I32), got_sc[4 * a : 4 * a + 112, :].bitcast(I32))
+        got_w = {}
+
+        def gather_words(a, h, dst):
+            nc.vector.tensor_copy(dst, tabs[a][:].bitcast(U32).indirect(half_offsets(l_tab, h)))
+            got_w[a, h] = dst
+
+        for a, h in ((0, 0), (1, 0), (2, 0), (2, 1)):
+            gather_words(a, h, keep.tile([P, HALF], U32, name="gotw%d%d" % (a, h), align_bytes=64)[:])
+        got_late = keep.tile([P, 2 * HALF], U32, tag="tablast", align_bytes=64)
+        for a in range(KP - 1):
+            gather_words(a, 1, got_late[:, half_cols(a)])
+
+        def first_product(b, h):
+            th = ring.tile([P, 4, PACK, P], F32, name="th", bufs=3)
+            at = ring.tile([P, 4, PACK, P], F32, name="at", bufs=3)
+            banks = []
+            for jl in range(4):
+                cols = slice((4 * h + jl) * P, (4 * h + jl + 1) * P)
+                acc = psum.tile([P, PASS], F32, name="acc", bufs=4)
+                for a in range(KP):
+                    plane = got_sc[:, cols] if a == 0 else moved[:, a - 1, cols]
+                    nc.tensor.matmul_mx(
+                        out=acc[:],
+                        lhsT=got_w[a, h][:, jl * P : (jl + 1) * P].bitcast(FP8X4),
+                        lhsT_scale=plane,
+                        rhs=w1_w[b][:, a, :].bitcast(FP4X4),
+                        rhs_scale=w1_sc[:, a, b * PASS : (b + 1) * PASS],
+                        start=(a == 0),
+                        stop=(a == KP - 1),
+                    )
+                banks.append(acc)
+            for slots in ((slice(0, 1), slice(1, PACK)) if (b, h) == (0, 0) else (slice(0, PACK),)):
+                for jl in range(4):
+                    nc.scalar.activation(th[:, jl, slots, :], banks[jl][:].rearrange("p (q t) -> p t q", t=PACK)[:, slots, :], ACT.Tanh)
+                for jl in range(4):
+                    nc.scalar.copy(at[:, jl, slots, :], banks[jl][:].rearrange("p (q t) -> p t q", t=PACK)[:, slots, :])
+            return th, at
+
+        def rows(src, b, t):
+            return src[b * PASS : (b + 1) * PASS, :].rearrange("(p t) c -> p t c", t=PACK)[:, t, :]
+
+        def load_mix(b, t):
+            mx = ring.tile([P, S], F32, name="mx", bufs=3)
+            nc.sync.dma_start(mx[:], rows(mix, b, t))
+            return mx
+
+        def load_page(b, t):
+            pg = wide([P, T2], F32, "page%d%d" % (b, t))
+            nc.sync.dma_start(pg[:], rows(page0, b, t))
+            return pg
+
+        wg = [keep.tile([P, S], F32, name="wg%d" % t) for t in range(PACK)]
+
+        def load_wg(t):
+            for g in range(4):
+                nc.sync.dma_start(wg[t][32 * g : 32 * g + 32, :], wgs.rearrange("(q t) j -> q t j", t=PACK)[:, t, :])
+
+        def make_h(b, t, h, mx, th, at, hh):
+            mt = psum.tile([P, 4, P], F32, name="mt")
+            for jl in range(4):
+                nc.tensor.transpose(mt[:, jl, :], mx[:, (4 * h + jl) * P : (4 * h + jl + 1) * P], ident[:])
+            nc.vector.tensor_tensor(th[:, :, t, :], mt[:], th[:, :, t, :], ALU.mult)
+            hb = psum.tile([P, 4, P], F32, name="hb")
+            for jl in range(4):
+                nc.tensor.matmul(hb[:, jl, :], at[:, jl, t, :], ident[:], start=(jl == 0), stop=False, is_transpose=True)
+            for jl in range(4):
+                nc.tensor.matmul(hb[:, jl, :], th[:, jl, t, :], ident[:], start=False, stop=(jl == 3), is_transpose=True)
+            nc.scalar.activation(hh[:, half_cols(h)], hb[:].rearrange("p a b -> p (a b)"), ACT.Copy, scale=gain_sb[:, b, t : t + 1])
+
+        def weave(dst, src):
+            nc.scalar.copy(dst.rearrange("p (c i) t -> p c t i", i=4), src.rearrange("p t (c i) -> p c t i", i=4))
+
+        def quantise(src, codes, scales, name, xi=None):
+            if xi is None:
+                xi = ring.tile([P, HALF * PACK], BF16, name=name, tag="xi", align_bytes=64)[:]
+            weave(xi.rearrange("p (c t) -> p c t", t=PACK), src)
+            nc.vector.quantize_mx(out=codes.bitcast(FP8X4), scales=scales, in_=xi)
+
+        w4_c = [keep.tile([P, N], U32, name="w4c%d" % b, align_bytes=64) for b in range(HP)]
+        w4_s = [keep.tile([P, N], U8, name="w4s%d" % b, align_bytes=64) for b in range(HP)]
+        x_c = {1: [keep.tile([P, HALF], U32, name="xc1%d" % m, align_bytes=64)[:] for m in range(2)]}
+        x_s = [[keep.tile([P, HALF], U8, name="xs%d%d" % (b, m), align_bytes=64) for m in range(2)] for b in range(HP)]
+
+        def do_w4(b):
+            raw = wide([P, PACK, N], F32, "w4raw%d" % b)
+            nc.sync.dma_start(raw[:], w4[b * PASS : (b + 1) * PASS, :].rearrange("(p t) n -> p t n", t=PACK))
+            quantise(raw[:], w4_c[b][:], w4_s[b][:], "w4i%d" % b)
+
+        def fetch(plane, pg, offsets):
+            nc.vector.tensor_copy(plane, pg[:].indirect(offsets))
+
+        def floor(plane, b, t):
+            nc.vector.tensor_scalar(plane, plane, low_sb[:, b, t : t + 1], None, ALU.max)
+
+        outs = {}
+
+        def load_out(q):
+            pg = wide([P, T2], F32, "outp%d" % q)
+            nc.sync.dma_start(pg[:], page1[q * P : (q + 1) * P, :])
+            outs[q] = pg
+
+        wgo_sb = keep.tile([P, M], F32)
+        units = [(b, t) for b in range(HP) for t in range(PACK)]
+        planes0 = keep.tile([P, PACK, M], BF16)
+        planes10 = keep.tile([P, PACK, HALF], BF16)
+        halves = {}
+        mixes = {units[0]: load_mix(0, 0)}
+        pages = {}
+        for u, (b, t) in enumerate(units):
+            last = u == len(units) - 1
+            if t == 0:
+                for h in range(2):
+                    halves[b, h] = first_product(b, h)
+            if last:
+                hh = keep.tile([P, S], F32, name="hlast", tag="late", align_bytes=64)
+            elif (b, t) == (1, 0):
+                hh = keep.tile([P, S], F32, name="hmid", tag="mid", align_bytes=64)
+            else:
+                hh = ring.tile([P, S], F32, name="hh", tag="hh", bufs=3)
+            for h in range(2):
+                make_h(b, t, h, mixes[b, t], halves[b, h][0], halves[b, h][1], hh)
+            if u > 1 and not last:
+                mixes[units[u + 1]] = load_mix(*units[u + 1])
+            pages[b, t] = load_page(b, t)
+            if u == 0:
+                nc.sync.dma_start(l_put[:], offs2)
+            if b == 0:
+                load_wg(t)
+            if u == 0:
+                nc.sync.dma_start(l_get[:], offs3)
+                mixes[units[1]] = load_mix(*units[1])
+            if u == 1:
+                mixes[units[2]] = load_mix(*units[2])
+                load_w1(1)
+            if u < 2:
+                for h in range(2):
+                    nc.vector.tensor_tensor(pages[b, t][:].indirect(half_offsets(l_put, h)), hh[:, half_cols(h)], wg[t][:, half_cols(h)], ALU.mult)
+            else:
+                nc.vector.tensor_tensor(pages[b, t][:].indirect(l_put[:]), hh[:], wg[t][:], ALU.mult)
+            if b == 0:
+                fetch(planes0[:, t, :], pages[b, t], l_get[:])
+                floor(planes0[:, t, :], b, t)
+            else:
+                fetch(planes10[:, t, :], pages[b, t], half_offsets(l_get, 0))
+                floor(planes10[:, t, :], b, t)
+            if b == 0 and t in (1, 2):
+                do_w4(t - 1)
+            if (b, t) == (1, 0):
+                xc0 = keep.tile([P, M], U32, tag="mid", align_bytes=64)
+                x_c[0] = [xc0[:, half_cols(m)] for m in range(2)]
+                for m in range(2):
+                    quantise(planes0[:, :, half_cols(m)], x_c[0][m], x_s[0][m][:], "xi0%d" % m)
+                nc.sync.dma_start(l_out[:], offs4)
+            if (b, t) == (1, 1):
+                load_out(0)
+                load_out(1)
+            if (b, t) == (1, 2):
+                nc.sync.dma_start(wgo_sb[:], wgo)
+                with nc.allow_non_contiguous_dma(reason="one target value a partition"):
+                    nc.sync.dma_start(target_sb[:], target.rearrange("(q p) -> p q", p=P))
+        load_out(2)
+        load_out(3)
+
+        late = keep.tile([P, 6 * HALF], BF16, tag="late", align_bytes=64)
+        quantise(planes10[:], x_c[1][0], x_s[1][0][:], "xi10", late[:, 2 * HALF : 6 * HALF])
+        planes11 = late[:, 0 : 4 * HALF].rearrange("p (t c) -> p t c", t=PACK)
+        for t in range(PACK):
+            fetch(planes11[:, t, :], pages[1, t], half_offsets(l_get, 1))
+        for t in range(PACK):
+            floor(planes11[:, t, :], 1, t)
+
+        def second(q, m):
+            acc = psum.tile([P, HALF], F32, name="acc", bufs=4)
+            for b in range(HP):
+                nc.tensor.matmul_mx(
+                    out=acc[:],
+                    lhsT=w4_c[b][:, q * P : (q + 1) * P].bitcast(FP8X4),
+                    lhsT_scale=w4_s[b][:, q * P : (q + 1) * P],
+                    rhs=x_c[b][m].bitcast(FP8X4),
+                    rhs_scale=x_s[b][m][:],
+                    start=(b == 0),
+                    stop=(b == HP - 1),
+                )
+            y = ring.tile([P, HALF], F32, name="y", tag="hh", bufs=3)
+            nc.scalar.activation(y[:], acc[:], ACT.Square, bias=target_sb[:, q : q + 1], scale=-1.0)
+            nc.vector.tensor_tensor(outs[q][:].indirect(half_offsets(l_out, m)), y[:], wgo_sb[:, half_cols(m)], ALU.mult)
+            if m == 1:
+                nc.sync.dma_start(out[q * P : (q + 1) * P, :], outs[q][:])
+
+        second(0, 0)
+        second(1, 0)
+        quantise(planes11, x_c[1][1], x_s[1][1][:], "xi11")
+        for q, m in ((0, 1), (1, 1), (2, 0), (2, 1), (3, 0), (3, 1)):
+            second(q, m)

@@ -57,34 +57,13 @@ def tile_list_overrun_valve_features_kernel(
         nc.vector.memset(tab_sc[:].bitcast(I32), 0)
         nc.vector.memset(moved[:].bitcast(I32), 0)
 
-        nc.sync.dma_start(l_tab[:], offs)
-        tabs = [wide([P, T], I32, "tab%d" % a) for a in range(KP - 1)]
-        tabs.append(keep.tile([P, T], I32, name="tab2", tag="tablast", align_bytes=64))
+        def rows(src, b, t):
+            return src[b * PASS : (b + 1) * PASS, :].rearrange("(p t) c -> p t c", t=PACK)[:, t, :]
 
-        def load_tab(a):
-            nc.sync.dma_start(tabs[a][:], tab_words[a].rearrange("p t i -> p (t i)").bitcast(I32))
-
-        load_tab(0)
-        staged = keep.tile([P, T // 4], I32)
-        for q in range(4):
-            eng = nc.sync if q < 2 else nc.scalar
-            live = slice(32 * q, 32 * q + 4 * KP)
-            eng.dma_start(staged[live, :], tab_scales[:, 4 * q : 4 * q + 4, :].bitcast(I32))
-            nc.vector.tensor_copy(tab_sc[live, :].bitcast(I32), staged[live, :])
-        load_tab(1)
-        load_tab(2)
-        for q in range(4):
-            nc.gpsimd.dma_start(
-                w1_sc[32 * q : 32 * q + 4, :, :].bitcast(I32),
-                w1_scales[:, 4 * q : 4 * q + 4, :].rearrange("a r c -> r a c").bitcast(I32),
-            )
-        ident = keep.tile([P, P], F32)
-        make_identity(nc, ident[:])
-        gain_sb = keep.tile([P, HP, PACK], F32)
-        low_sb = keep.tile([P, HP, PACK], F32)
-        target_sb = keep.tile([P, NQ], F32)
-        nc.gpsimd.dma_start(gain_sb[:], gain.rearrange("(b p t) -> p b t", b=HP, t=PACK))
-        nc.gpsimd.dma_start(low_sb[:], low.rearrange("(b p t) -> p b t", b=HP, t=PACK))
+        def load_mix(b, t):
+            mx = ring.tile([P, S], F32, name="mx", bufs=3)
+            nc.sync.dma_start(mx[:], rows(mix, b, t))
+            return mx
 
         w1_w = [keep.tile([P, KP, 2 * PASS], U8, name="w1w%d" % b, align_bytes=64) for b in range(HP)]
 
@@ -94,7 +73,34 @@ def tile_list_overrun_valve_features_kernel(
                 w1_words[:, :, 2 * PASS * b : 2 * PASS * (b + 1)].rearrange("a p c -> p a c").bitcast(I32),
             )
 
+        tabs = [wide([P, T], I32, "tab%d" % a) for a in range(KP - 1)]
+        tabs.append(keep.tile([P, T], I32, name="tab2", tag="tablast", align_bytes=64))
+
+        def load_tab(a):
+            nc.sync.dma_start(tabs[a][:], tab_words[a].rearrange("p t i -> p (t i)").bitcast(I32))
+
+        staged = keep.tile([P, T // 4], I32, tag="xc10", align_bytes=64)
+        for q in range(4):
+            eng = nc.sync if q < 2 else nc.scalar
+            live = slice(32 * q, 32 * q + 4 * KP)
+            eng.dma_start(staged[live, :], tab_scales[:, 4 * q : 4 * q + 4, :].bitcast(I32))
+            nc.vector.tensor_copy(tab_sc[live, :].bitcast(I32), staged[live, :])
+        nc.sync.dma_start(l_tab[:], offs)
+        load_tab(0)
         load_w1(0)
+        load_tab(1)
+        load_tab(2)
+        mixes = {(0, 0): load_mix(0, 0)}
+        for q in range(4):
+            nc.scalar.dma_start(
+                w1_sc[32 * q : 32 * q + 4, :, :].bitcast(I32),
+                w1_scales[:, 4 * q : 4 * q + 4, :].rearrange("a r c -> r a c").bitcast(I32),
+            )
+        ident = keep.tile([P, P], F32)
+        make_identity(nc, ident[:])
+        gain_sb = keep.tile([P, HP, PACK], F32)
+        low_sb = keep.tile([P, HP, PACK], F32)
+        target_sb = keep.tile([P, NQ], F32)
 
         got_sc = keep.tile([P, S], U8, align_bytes=64)
         nc.vector.tensor_copy(got_sc[:], tab_sc[:].indirect(l_tab[:]))
@@ -106,11 +112,10 @@ def tile_list_overrun_valve_features_kernel(
             nc.vector.tensor_copy(dst, tabs[a][:].bitcast(U32).indirect(half_offsets(l_tab, h)))
             got_w[a, h] = dst
 
-        for a, h in ((0, 0), (1, 0), (2, 0), (2, 1)):
+        for a, h in ((0, 0), (1, 0), (2, 0), (0, 1), (2, 1)):
             gather_words(a, h, keep.tile([P, HALF], U32, name="gotw%d%d" % (a, h), align_bytes=64)[:])
-        got_late = keep.tile([P, 2 * HALF], U32, tag="tablast", align_bytes=64)
-        for a in range(KP - 1):
-            gather_words(a, 1, got_late[:, half_cols(a)])
+        got_late = keep.tile([P, HALF], U32, tag="tablast", align_bytes=64)
+        gather_words(1, 1, got_late[:])
 
         def first_product(b, h):
             th = ring.tile([P, 4, PACK, P], F32, name="th", bufs=3)
@@ -131,27 +136,21 @@ def tile_list_overrun_valve_features_kernel(
                         stop=(a == KP - 1),
                     )
                 banks.append(acc)
-            for slots in ((slice(0, 1), slice(1, PACK)) if (b, h) == (0, 0) else (slice(0, PACK),)):
-                for jl in range(4):
-                    nc.scalar.activation(th[:, jl, slots, :], banks[jl][:].rearrange("p (q t) -> p t q", t=PACK)[:, slots, :], ACT.Tanh)
-                for jl in range(4):
-                    nc.scalar.copy(at[:, jl, slots, :], banks[jl][:].rearrange("p (q t) -> p t q", t=PACK)[:, slots, :])
-            return th, at
+            return th, at, banks
 
-        def rows(src, b, t):
-            return src[b * PASS : (b + 1) * PASS, :].rearrange("(p t) c -> p t c", t=PACK)[:, t, :]
-
-        def load_mix(b, t):
-            mx = ring.tile([P, S], F32, name="mx", bufs=3)
-            nc.sync.dma_start(mx[:], rows(mix, b, t))
-            return mx
+        def empty(half, slots):
+            th, at, banks = half
+            for jl in range(4):
+                nc.scalar.activation(th[:, jl, slots, :], banks[jl][:].rearrange("p (q t) -> p t q", t=PACK)[:, slots, :], ACT.Tanh)
+            for jl in range(4):
+                nc.scalar.copy(at[:, jl, slots, :], banks[jl][:].rearrange("p (q t) -> p t q", t=PACK)[:, slots, :])
 
         def load_page(b, t):
             pg = wide([P, T2], F32, "page%d%d" % (b, t))
             nc.sync.dma_start(pg[:], rows(page0, b, t))
             return pg
 
-        wg = [keep.tile([P, S], F32, name="wg%d" % t) for t in range(PACK)]
+        wg = [keep.tile([P, S], F32, name="wg%d" % t, tag="wg%d" % t, align_bytes=64) for t in range(PACK)]
 
         def load_wg(t):
             for g in range(4):
@@ -172,15 +171,20 @@ def tile_list_overrun_valve_features_kernel(
         def weave(dst, src):
             nc.scalar.copy(dst.rearrange("p (c i) t -> p c t i", i=4), src.rearrange("p t (c i) -> p c t i", i=4))
 
-        def quantise(src, codes, scales, name, xi=None):
-            if xi is None:
-                xi = ring.tile([P, HALF * PACK], BF16, name=name, tag="xi", align_bytes=64)[:]
+        def weave_ring(src, name):
+            xi = ring.tile([P, HALF * PACK], BF16, name=name, tag="xi", align_bytes=64)[:]
             weave(xi.rearrange("p (c t) -> p c t", t=PACK), src)
+            return xi
+
+        def quantise_woven(xi, codes, scales):
             nc.vector.quantize_mx(out=codes.bitcast(FP8X4), scales=scales, in_=xi)
+
+        def quantise(src, codes, scales, name):
+            quantise_woven(weave_ring(src, name), codes, scales)
 
         w4_c = [keep.tile([P, N], U32, name="w4c%d" % b, align_bytes=64) for b in range(HP)]
         w4_s = [keep.tile([P, N], U8, name="w4s%d" % b, align_bytes=64) for b in range(HP)]
-        x_c = {1: [keep.tile([P, HALF], U32, name="xc1%d" % m, align_bytes=64)[:] for m in range(2)]}
+        x_c = {1: [keep.tile([P, HALF], U32, name="xc1%d" % m, tag="xc1%d" % m, align_bytes=64)[:] for m in range(2)]}
         x_s = [[keep.tile([P, HALF], U8, name="xs%d%d" % (b, m), align_bytes=64) for m in range(2)] for b in range(HP)]
 
         def do_w4(b):
@@ -203,73 +207,115 @@ def tile_list_overrun_valve_features_kernel(
 
         wgo_sb = keep.tile([P, M], F32)
         units = [(b, t) for b in range(HP) for t in range(PACK)]
-        planes0 = keep.tile([P, PACK, M], BF16)
-        planes10 = keep.tile([P, PACK, HALF], BF16)
+        n_units = len(units)
+        SLOT = 2 * S
+        arena = keep.tile([P, 10 * S + S // 2], F32, align_bytes=64)
+        arena16 = arena[:].bitcast(BF16)
+
+        def run16(slot, start, width):
+            return arena16[:, slot * SLOT + start : slot * SLOT + start + width]
+
+        def planes16(slot, start, width):
+            base = slot * SLOT + start + width - SLOT
+            return arena16[:, base : base + PACK * SLOT].rearrange("p (t c) -> p t c", t=PACK)[:, :, SLOT - width : SLOT]
+
+        def raw(u):
+            return run16(u + 1, 0, M) if u < PACK else run16(u + 1, HALF, HALF)
+
+        def floored(u):
+            return run16(u + 2, M, M) if u < PACK else run16(u + 2, 0, HALF)
+
+        def fetch_unit(u):
+            fetch(raw(u), pages[units[u]], l_get[:] if u < PACK else half_offsets(l_get, 0))
+
+        def floor_unit(u):
+            b, t = units[u]
+            nc.vector.tensor_scalar(floored(u), raw(u), low_sb[:, b, t : t + 1], None, ALU.max)
+
+        x_c[0] = {}
         halves = {}
-        mixes = {units[0]: load_mix(0, 0)}
-        pages = {}
+        nc.sync.dma_start(gain_sb[:], gain.rearrange("(b p t) -> p b t", b=HP, t=PACK))
+        nc.sync.dma_start(l_put[:], offs2)
+        pages = {units[0]: load_page(0, 0)}
+        load_wg(0)
+        mixes[units[1]] = load_mix(0, 1)
+
+        def h_slot(u):
+            return arena[:, u * S : (u + 1) * S]
+
+        def h_half(u, h):
+            b, t = units[u]
+            make_h(b, t, h, mixes[b, t], halves[b, h][0], halves[b, h][1], h_slot(u))
+
+        halves[0, 0] = first_product(0, 0)
+        empty(halves[0, 0], slice(0, 1))
+        h_half(0, 0)
+        empty(halves[0, 0], slice(1, PACK))
+        h_half(1, 0)
+        halves[0, 1] = first_product(0, 1)
+        empty(halves[0, 1], slice(0, PACK))
+        woven = {}
         for u, (b, t) in enumerate(units):
-            last = u == len(units) - 1
-            if t == 0:
+            last = u == n_units - 1
+            if u == PACK:
                 for h in range(2):
                     halves[b, h] = first_product(b, h)
-            if last:
-                hh = keep.tile([P, S], F32, name="hlast", tag="late", align_bytes=64)
-            elif (b, t) == (1, 0):
-                hh = keep.tile([P, S], F32, name="hmid", tag="mid", align_bytes=64)
-            else:
-                hh = ring.tile([P, S], F32, name="hh", tag="hh", bufs=3)
-            for h in range(2):
-                make_h(b, t, h, mixes[b, t], halves[b, h][0], halves[b, h][1], hh)
+                    empty(halves[b, h], slice(0, PACK))
+            hh = h_slot(u)
+            for h in range(1 if u < 2 else 0, 2):
+                h_half(u, h)
             if u > 1 and not last:
                 mixes[units[u + 1]] = load_mix(*units[u + 1])
-            pages[b, t] = load_page(b, t)
-            if u == 0:
-                nc.sync.dma_start(l_put[:], offs2)
-            if b == 0:
+            if u > 0:
+                pages[b, t] = load_page(b, t)
+            if b == 0 and t > 0:
                 load_wg(t)
-            if u == 0:
-                nc.sync.dma_start(l_get[:], offs3)
-                mixes[units[1]] = load_mix(*units[1])
             if u == 1:
+                nc.sync.dma_start(l_get[:], offs3)
+                nc.sync.dma_start(low_sb[:], low.rearrange("(b p t) -> p b t", b=HP, t=PACK))
                 mixes[units[2]] = load_mix(*units[2])
                 load_w1(1)
             if u < 2:
                 for h in range(2):
                     nc.vector.tensor_tensor(pages[b, t][:].indirect(half_offsets(l_put, h)), hh[:, half_cols(h)], wg[t][:, half_cols(h)], ALU.mult)
             else:
-                nc.vector.tensor_tensor(pages[b, t][:].indirect(l_put[:]), hh[:], wg[t][:], ALU.mult)
-            if b == 0:
-                fetch(planes0[:, t, :], pages[b, t], l_get[:])
-                floor(planes0[:, t, :], b, t)
-            else:
-                fetch(planes10[:, t, :], pages[b, t], half_offsets(l_get, 0))
-                floor(planes10[:, t, :], b, t)
-            if b == 0 and t in (1, 2):
-                do_w4(t - 1)
-            if (b, t) == (1, 0):
-                xc0 = keep.tile([P, M], U32, tag="mid", align_bytes=64)
-                x_c[0] = [xc0[:, half_cols(m)] for m in range(2)]
-                for m in range(2):
-                    quantise(planes0[:, :, half_cols(m)], x_c[0][m], x_s[0][m][:], "xi0%d" % m)
+                nc.vector.tensor_tensor(pages[b, t][:].indirect(l_put[:]), hh, wg[t][:], ALU.mult)
+            if u >= 2:
+                floor_unit(u - 2)
+            if u >= 1:
+                fetch_unit(u - 1)
+            if u in (1, 2):
+                do_w4(u - 1)
+            if u == 4:
                 nc.sync.dma_start(l_out[:], offs4)
-            if (b, t) == (1, 1):
+            if u == 5:
+                for m in range(2):
+                    woven[m] = weave_ring(planes16(2, M + m * HALF, HALF), "xi0%d" % m)
                 load_out(0)
                 load_out(1)
-            if (b, t) == (1, 2):
+            if u == 6:
+                x_c[0][0] = keep.tile([P, HALF], U32, name="xc00", tag="wg2", align_bytes=64)[:]
+                quantise_woven(woven[0], x_c[0][0], x_s[0][0][:])
                 nc.sync.dma_start(wgo_sb[:], wgo)
                 with nc.allow_non_contiguous_dma(reason="one target value a partition"):
                     nc.sync.dma_start(target_sb[:], target.rearrange("(q p) -> p q", p=P))
         load_out(2)
         load_out(3)
 
-        late = keep.tile([P, 6 * HALF], BF16, tag="late", align_bytes=64)
-        quantise(planes10[:], x_c[1][0], x_s[1][0][:], "xi10", late[:, 2 * HALF : 6 * HALF])
-        planes11 = late[:, 0 : 4 * HALF].rearrange("p (t c) -> p t c", t=PACK)
+        fetch_unit(7)
+        floor_unit(6)
+        floor_unit(7)
+        xi10 = run16(9, 768, PACK * HALF)
+        weave(xi10.rearrange("p (c t) -> p c t", t=PACK), planes16(6, 0, HALF))
+        x_c[0][1] = keep.tile([P, HALF], U32, name="xc01", tag="wg3", align_bytes=64)[:]
+        quantise_woven(woven[1], x_c[0][1], x_s[0][1][:])
+        quantise_woven(xi10, x_c[1][0], x_s[1][0][:])
+        planes11 = planes16(7, HALF, HALF)
         for t in range(PACK):
-            fetch(planes11[:, t, :], pages[1, t], half_offsets(l_get, 1))
+            fetch(run16(7 + t, HALF, HALF), pages[1, t], half_offsets(l_get, 1))
         for t in range(PACK):
-            floor(planes11[:, t, :], 1, t)
+            floor(run16(7 + t, HALF, HALF), 1, t)
+        ys = [arena[:, i * HALF : (i + 1) * HALF] for i in range(4)]
 
         def second(q, m):
             acc = psum.tile([P, HALF], F32, name="acc", bufs=4)
@@ -283,9 +329,9 @@ def tile_list_overrun_valve_features_kernel(
                     start=(b == 0),
                     stop=(b == HP - 1),
                 )
-            y = ring.tile([P, HALF], F32, name="y", tag="hh", bufs=3)
-            nc.scalar.activation(y[:], acc[:], ACT.Square, bias=target_sb[:, q : q + 1], scale=-1.0)
-            nc.vector.tensor_tensor(outs[q][:].indirect(half_offsets(l_out, m)), y[:], wgo_sb[:, half_cols(m)], ALU.mult)
+            y = ys[(2 * q + m) % 4]
+            nc.scalar.activation(y, acc[:], ACT.Square, bias=target_sb[:, q : q + 1], scale=-1.0)
+            nc.vector.tensor_tensor(outs[q][:].indirect(half_offsets(l_out, m)), y, wgo_sb[:, half_cols(m)], ALU.mult)
             if m == 1:
                 nc.sync.dma_start(out[q * P : (q + 1) * P, :], outs[q][:])
 

@@ -90,7 +90,6 @@ def tile_list_overrun_valve_features_kernel(
         load_w1(0)
         load_tab(1)
         load_tab(2)
-        mixes = {(0, 0): load_mix(0, 0)}
         for q in range(4):
             nc.scalar.dma_start(
                 w1_sc[32 * q : 32 * q + 4, :, :].bitcast(I32),
@@ -102,10 +101,12 @@ def tile_list_overrun_valve_features_kernel(
         low_sb = keep.tile([P, HP, PACK], F32)
         target_sb = keep.tile([P, NQ], F32)
 
+        nc.sync.dma_start(gain_sb[:], gain.rearrange("(b p t) -> p b t", b=HP, t=PACK))
+        nc.sync.dma_start(l_put[:], offs2)
         got_sc = keep.tile([P, S], U8, align_bytes=64)
         nc.vector.tensor_copy(got_sc[:], tab_sc[:].indirect(l_tab[:]))
         for a in range(1, KP):
-            nc.scalar.dma_start(moved[0:112, a - 1, :].bitcast(I32), got_sc[4 * a : 4 * a + 112, :].bitcast(I32))
+            nc.sync.dma_start(moved[0:112, a - 1, :].bitcast(I32), got_sc[4 * a : 4 * a + 112, :].bitcast(I32))
         got_w = {}
 
         def gather_words(a, h, dst):
@@ -138,12 +139,13 @@ def tile_list_overrun_valve_features_kernel(
                 banks.append(acc)
             return th, at, banks
 
-        def empty(half, slots):
+        def empty(half, slots, by_bank):
             th, at, banks = half
-            for jl in range(4):
-                nc.scalar.activation(th[:, jl, slots, :], banks[jl][:].rearrange("p (q t) -> p t q", t=PACK)[:, slots, :], ACT.Tanh)
-            for jl in range(4):
-                nc.scalar.copy(at[:, jl, slots, :], banks[jl][:].rearrange("p (q t) -> p t q", t=PACK)[:, slots, :])
+            for group in ([[jl] for jl in range(4)] if by_bank else [range(4)]):
+                for jl in group:
+                    nc.scalar.activation(th[:, jl, slots, :], banks[jl][:].rearrange("p (q t) -> p t q", t=PACK)[:, slots, :], ACT.Tanh)
+                for jl in group:
+                    nc.scalar.copy(at[:, jl, slots, :], banks[jl][:].rearrange("p (q t) -> p t q", t=PACK)[:, slots, :])
 
         def load_page(b, t):
             pg = wide([P, T2], F32, "page%d%d" % (b, t))
@@ -234,8 +236,7 @@ def tile_list_overrun_valve_features_kernel(
 
         x_c[0] = {}
         halves = {}
-        nc.sync.dma_start(gain_sb[:], gain.rearrange("(b p t) -> p b t", b=HP, t=PACK))
-        nc.sync.dma_start(l_put[:], offs2)
+        mixes = {units[0]: load_mix(0, 0)}
         pages = {units[0]: load_page(0, 0)}
         load_wg(0)
         mixes[units[1]] = load_mix(0, 1)
@@ -248,21 +249,24 @@ def tile_list_overrun_valve_features_kernel(
             make_h(b, t, h, mixes[b, t], halves[b, h][0], halves[b, h][1], h_slot(u))
 
         halves[0, 0] = first_product(0, 0)
-        empty(halves[0, 0], slice(0, 1))
+        empty(halves[0, 0], slice(0, 1), False)
         h_half(0, 0)
-        empty(halves[0, 0], slice(1, PACK))
+        empty(halves[0, 0], slice(1, PACK), True)
         h_half(1, 0)
         halves[0, 1] = first_product(0, 1)
-        empty(halves[0, 1], slice(0, PACK))
+        empty(halves[0, 1], slice(0, 2), False)
+        h_half(0, 1)
+        h_half(1, 1)
+        empty(halves[0, 1], slice(2, PACK), True)
         woven = {}
         for u, (b, t) in enumerate(units):
             last = u == n_units - 1
             if u == PACK:
                 for h in range(2):
                     halves[b, h] = first_product(b, h)
-                    empty(halves[b, h], slice(0, PACK))
+                    empty(halves[b, h], slice(0, PACK), True)
             hh = h_slot(u)
-            for h in range(1 if u < 2 else 0, 2):
+            for h in range(2 if u >= 2 else 0):
                 h_half(u, h)
             if u > 1 and not last:
                 mixes[units[u + 1]] = load_mix(*units[u + 1])

@@ -155,7 +155,7 @@ def tile_list_overrun_valve_features_kernel(
         wg = [keep.tile([P, S], F32, name="wg%d" % t, tag="wg%d" % t, align_bytes=64) for t in range(PACK)]
 
         def load_wg(t):
-            for g in range(4):
+            for g in (0, 2, 1, 3):
                 nc.sync.dma_start(wg[t][32 * g : 32 * g + 32, :], wgs.rearrange("(q t) j -> q t j", t=PACK)[:, t, :])
 
         def make_h(b, t, h, mx, th, at, hh):
@@ -278,6 +278,7 @@ def tile_list_overrun_valve_features_kernel(
                 nc.sync.dma_start(l_get[:], offs3)
                 nc.sync.dma_start(low_sb[:], low.rearrange("(b p t) -> p b t", b=HP, t=PACK))
                 mixes[units[2]] = load_mix(*units[2])
+            if u == 2:
                 load_w1(1)
             if u < 2:
                 for h in range(2):
@@ -288,8 +289,8 @@ def tile_list_overrun_valve_features_kernel(
                 floor_unit(u - 2)
             if u >= 1:
                 fetch_unit(u - 1)
-            if u in (1, 2):
-                do_w4(u - 1)
+            if u in (3, 4):
+                do_w4(u - 3)
             if u == 4:
                 nc.sync.dma_start(l_out[:], offs4)
             if u == 5:
@@ -319,7 +320,6 @@ def tile_list_overrun_valve_features_kernel(
             fetch(run16(7 + t, HALF, HALF), pages[1, t], half_offsets(l_get, 1))
         for t in range(PACK):
             floor(run16(7 + t, HALF, HALF), 1, t)
-        ys = [arena[:, i * HALF : (i + 1) * HALF] for i in range(4)]
 
         def second(q, m):
             acc = psum.tile([P, HALF], F32, name="acc", bufs=4)
@@ -333,9 +333,12 @@ def tile_list_overrun_valve_features_kernel(
                     start=(b == 0),
                     stop=(b == HP - 1),
                 )
-            y = ys[(2 * q + m) % 4]
+            y = arena[:, q * M + m * HALF : q * M + (m + 1) * HALF]
             nc.scalar.activation(y, acc[:], ACT.Square, bias=target_sb[:, q : q + 1], scale=-1.0)
-            nc.vector.tensor_tensor(outs[q][:].indirect(half_offsets(l_out, m)), y, wgo_sb[:, half_cols(m)], ALU.mult)
+            if q < 2:
+                nc.vector.tensor_tensor(outs[q][:].indirect(half_offsets(l_out, m)), y, wgo_sb[:, half_cols(m)], ALU.mult)
+            elif m == 1:
+                nc.vector.tensor_tensor(outs[q][:].indirect(l_out[:]), arena[:, q * M : (q + 1) * M], wgo_sb[:], ALU.mult)
             if m == 1:
                 nc.sync.dma_start(out[q * P : (q + 1) * P, :], outs[q][:])
 

@@ -119,8 +119,9 @@ def tile_list_overrun_valve_features_kernel(
         gather_words(1, 1, got_late[:])
 
         def first_product(b, h):
-            th = ring.tile([P, 4, PACK, P], F32, name="th", bufs=3)
-            at = ring.tile([P, 4, PACK, P], F32, name="at", bufs=3)
+            place = (2 * b + h) % 3
+            th = keep.tile([P, 4, PACK, P], F32, name="th%d%d" % (b, h), tag="th%d" % place, align_bytes=64)
+            at = keep.tile([P, 4, PACK, P], F32, name="at%d%d" % (b, h), tag="at%d" % place, align_bytes=64)
             banks = []
             for jl in range(4):
                 cols = slice((4 * h + jl) * P, (4 * h + jl + 1) * P)
@@ -162,13 +163,20 @@ def tile_list_overrun_valve_features_kernel(
             mt = psum.tile([P, 4, P], F32, name="mt")
             for jl in range(4):
                 nc.tensor.transpose(mt[:, jl, :], mx[:, (4 * h + jl) * P : (4 * h + jl + 1) * P], ident[:])
-            nc.vector.tensor_tensor(th[:, :, t, :], mt[:], th[:, :, t, :], ALU.mult)
+            if (b, t) < (0, 2):
+                nc.vector.tensor_tensor(th[:, :, t, :], mt[:], th[:, :, t, :], ALU.mult)
+            else:
+                turned = mx[:, half_cols(h)].rearrange("p (a b) -> p a b", a=4)
+                nc.scalar.copy(turned, mt[:])
+                nc.gpsimd.tensor_tensor(th[:, :, t, :], turned, th[:, :, t, :], ALU.mult)
             hb = psum.tile([P, 4, P], F32, name="hb")
             for jl in range(4):
                 nc.tensor.matmul(hb[:, jl, :], at[:, jl, t, :], ident[:], start=(jl == 0), stop=False, is_transpose=True)
             for jl in range(4):
                 nc.tensor.matmul(hb[:, jl, :], th[:, jl, t, :], ident[:], start=False, stop=(jl == 3), is_transpose=True)
             nc.scalar.activation(hh[:, half_cols(h)], hb[:].rearrange("p a b -> p (a b)"), ACT.Copy, scale=gain_sb[:, b, t : t + 1])
+            if (b, t) < (1, 2):
+                nc.gpsimd.tensor_tensor(hh[:, half_cols(h)], hh[:, half_cols(h)], wg[t][:, half_cols(h)], ALU.mult)
 
         def weave(dst, src):
             nc.scalar.copy(dst.rearrange("p (c i) t -> p c t i", i=4), src.rearrange("p t (c i) -> p c t i", i=4))
@@ -240,6 +248,8 @@ def tile_list_overrun_valve_features_kernel(
         pages = {units[0]: load_page(0, 0)}
         load_wg(0)
         mixes[units[1]] = load_mix(0, 1)
+        pages[units[1]] = load_page(0, 1)
+        load_wg(1)
 
         def h_slot(u):
             return arena[:, u * S : (u + 1) * S]
@@ -266,14 +276,18 @@ def tile_list_overrun_valve_features_kernel(
                     halves[b, h] = first_product(b, h)
                     empty(halves[b, h], slice(0, PACK), True)
             hh = h_slot(u)
+            if u in (2, 3):
+                load_wg(t)
             for h in range(2 if u >= 2 else 0):
                 h_half(u, h)
+            if last:
+                for m, tag in ((0, "th2"), (1, "th0")):
+                    woven[m] = keep.tile([P, HALF * PACK], BF16, name="xi0%d" % m, tag=tag, align_bytes=64)[:]
+                    weave(woven[m].rearrange("p (c t) -> p c t", t=PACK), planes16(2, M + m * HALF, HALF))
             if u > 1 and not last:
                 mixes[units[u + 1]] = load_mix(*units[u + 1])
-            if u > 0:
+            if u > 1:
                 pages[b, t] = load_page(b, t)
-            if b == 0 and t > 0:
-                load_wg(t)
             if u == 1:
                 nc.sync.dma_start(l_get[:], offs3)
                 nc.sync.dma_start(low_sb[:], low.rearrange("(b p t) -> p b t", b=HP, t=PACK))
@@ -282,7 +296,9 @@ def tile_list_overrun_valve_features_kernel(
                 load_w1(1)
             if u < 2:
                 for h in range(2):
-                    nc.vector.tensor_tensor(pages[b, t][:].indirect(half_offsets(l_put, h)), hh[:, half_cols(h)], wg[t][:, half_cols(h)], ALU.mult)
+                    nc.vector.tensor_copy(pages[b, t][:].indirect(half_offsets(l_put, h)), hh[:, half_cols(h)])
+            elif u < 6:
+                nc.vector.tensor_copy(pages[b, t][:].indirect(l_put[:]), hh)
             else:
                 nc.vector.tensor_tensor(pages[b, t][:].indirect(l_put[:]), hh, wg[t][:], ALU.mult)
             if u >= 2:
@@ -294,13 +310,9 @@ def tile_list_overrun_valve_features_kernel(
             if u == 4:
                 nc.sync.dma_start(l_out[:], offs4)
             if u == 5:
-                for m in range(2):
-                    woven[m] = weave_ring(planes16(2, M + m * HALF, HALF), "xi0%d" % m)
                 load_out(0)
                 load_out(1)
             if u == 6:
-                x_c[0][0] = keep.tile([P, HALF], U32, name="xc00", tag="wg2", align_bytes=64)[:]
-                quantise_woven(woven[0], x_c[0][0], x_s[0][0][:])
                 nc.sync.dma_start(wgo_sb[:], wgo)
                 with nc.allow_non_contiguous_dma(reason="one target value a partition"):
                     nc.sync.dma_start(target_sb[:], target.rearrange("(q p) -> p q", p=P))
@@ -312,6 +324,8 @@ def tile_list_overrun_valve_features_kernel(
         floor_unit(7)
         xi10 = run16(9, 768, PACK * HALF)
         weave(xi10.rearrange("p (c t) -> p c t", t=PACK), planes16(6, 0, HALF))
+        x_c[0][0] = keep.tile([P, HALF], U32, name="xc00", tag="wg2", align_bytes=64)[:]
+        quantise_woven(woven[0], x_c[0][0], x_s[0][0][:])
         x_c[0][1] = keep.tile([P, HALF], U32, name="xc01", tag="wg3", align_bytes=64)[:]
         quantise_woven(woven[1], x_c[0][1], x_s[0][1][:])
         quantise_woven(xi10, x_c[1][0], x_s[1][0][:])

from contextlib import ExitStack

import concourse.mybir as mybir
from concourse.masks import make_identity

K, H, N, T, S, M, T2 = 1536, 1024, 512, 2048, 1024, 1024, 2048
FLOPS = 2 * K * H * S + 2 * H * N * M

F32 = mybir.dt.float32
BF16 = mybir.dt.bfloat16
I32 = mybir.dt.int32
U32 = mybir.dt.uint32
U16 = mybir.dt.uint16
U8 = mybir.dt.uint8
FP8X4 = mybir.dt.float8_e4m3fn_x4
FP4X4 = mybir.dt.float4_e2m1fn_x4
ACT = mybir.ActivationFunctionType
ALU = mybir.AluOpType

P = 128
PACK = 4
PASS = P * PACK
HALF = 512
KP = K // PASS
HP = H // PASS
NQ = N // P
WIDE_BUFS = 8


def half_cols(h):
    return slice(h * HALF, (h + 1) * HALF)


def half_offsets(tile, h):
    return tile[:, h * HALF // 16 : (h + 1) * HALF // 16]


def tile_list_overrun_valve_features_kernel(
    tc, tab_words, tab_scales, offs, offs2, offs3, offs4, w1_words, w1_scales, mix, gain, wgs, page0, low, w4, target, wgo, page1, out
):
    nc = tc.nc
    with ExitStack() as ctx:
        keep = ctx.enter_context(tc.tile_pool(name="keep", bufs=1))
        ring = ctx.enter_context(tc.tile_pool(name="ring", bufs=2))
        psum = ctx.enter_context(tc.psum_pool(name="psum", bufs=2))

        def wide(shape, dtype, name):
            return ring.tile(shape, dtype, name=name, tag="wide", bufs=WIDE_BUFS)

        lists = [keep.tile([P, S // 16], U16, name="list%d" % i) for i in range(4)]
        l_tab, l_put, l_get, l_out = lists

        tab_sc = keep.tile([P, T], U8)
        w1_sc = keep.tile([P, KP, H], U8, align_bytes=64)
        moved = keep.tile([P, KP - 1, S], U8, align_bytes=64)
        nc.gpsimd.memset(w1_sc[:].bitcast(I32), 0)
        nc.vector.memset(tab_sc[:].bitcast(I32), 0)
        nc.vector.memset(moved[:].bitcast(I32), 0)

        def rows(src, b, t):
            return src[b * PASS : (b + 1) * PASS, :].rearrange("(p t) c -> p t c", t=PACK)[:, t, :]

        def load_mix(b, t):
            mx = ring.tile([P, S], F32, name="mx", bufs=3)
            nc.sync.dma_start(mx[:], rows(mix, b, t))
            return mx

        w1_w = [keep.tile([P, KP, 2 * PASS], U8, name="w1w%d" % b, align_bytes=64) for b in range(HP)]

        def load_w1(b):
            nc.sync.dma_start(
                w1_w[b][:].bitcast(I32),
                w1_words[:, :, 2 * PASS * b : 2 * PASS * (b + 1)].rearrange("a p c -> p a c").bitcast(I32),
            )

        tabs = [wide([P, T], I32, "tab%d" % a) for a in range(KP - 1)]
        tabs.append(keep.tile([P, T], I32, name="tab2", tag="tablast", align_bytes=64))

        def load_tab(a):
            nc.sync.dma_start(tabs[a][:], tab_words[a].rearrange("p t i -> p (t i)").bitcast(I32))

        staged = keep.tile([P, T // 4], I32, tag="xc10", align_bytes=64)
        for q in range(4):
            eng = nc.sync if q < 2 else nc.scalar
            live = slice(32 * q, 32 * q + 4 * KP)
            eng.dma_start(staged[live, :], tab_scales[:, 4 * q : 4 * q + 4, :].bitcast(I32))
            nc.vector.tensor_copy(tab_sc[live, :].bitcast(I32), staged[live, :])
        nc.sync.dma_start(l_tab[:], offs)
        load_tab(0)
        load_w1(0)
        load_tab(1)
        load_tab(2)
        for q in range(4):
            nc.scalar.dma_start(
                w1_sc[32 * q : 32 * q + 4, :, :].bitcast(I32),
                w1_scales[:, 4 * q : 4 * q + 4, :].rearrange("a r c -> r a c").bitcast(I32),
            )
        ident = keep.tile([P, P], F32)
        make_identity(nc, ident[:])
        gain_sb = keep.tile([P, HP, PACK], F32)
        low_sb = keep.tile([P, HP, PACK], F32)
        target_sb = keep.tile([P, NQ], F32)

        nc.sync.dma_start(gain_sb[:], gain.rearrange("(b p t) -> p b t", b=HP, t=PACK))
        nc.sync.dma_start(l_put[:], offs2)
        got_sc = keep.tile([P, S], U8, align_bytes=64)
        nc.vector.tensor_copy(got_sc[:], tab_sc[:].indirect(l_tab[:]))
        for a in range(1, KP):
            nc.sync.dma_start(moved[0:112, a - 1, :].bitcast(I32), got_sc[4 * a : 4 * a + 112, :].bitcast(I32))
        got_w = {}

        def gather_words(a, h, dst):
            nc.vector.tensor_copy(dst, tabs[a][:].bitcast(U32).indirect(half_offsets(l_tab, h)))
            got_w[a, h] = dst

        for a, h in ((0, 0), (1, 0), (2, 0), (0, 1), (2, 1)):
            gather_words(a, h, keep.tile([P, HALF], U32, name="gotw%d%d" % (a, h), align_bytes=64)[:])
        got_late = keep.tile([P, HALF], U32, tag="tablast", align_bytes=64)
        gather_words(1, 1, got_late[:])

        def first_product(b, h):
            place = (2 * b + h) % 3
            th = keep.tile([P, 4, PACK, P], F32, name="th%d%d" % (b, h), tag="th%d" % place, align_bytes=64)
            at = keep.tile([P, 4, PACK, P], F32, name="at%d%d" % (b, h), tag="at%d" % place, align_bytes=64)
            banks = []
            for jl in range(4):
                cols = slice((4 * h + jl) * P, (4 * h + jl + 1) * P)
                acc = psum.tile([P, PASS], F32, name="acc", bufs=4)
                for a in range(KP):
                    plane = got_sc[:, cols] if a == 0 else moved[:, a - 1, cols]
                    nc.tensor.matmul_mx(
                        out=acc[:],
                        lhsT=got_w[a, h][:, jl * P : (jl + 1) * P].bitcast(FP8X4),
                        lhsT_scale=plane,
                        rhs=w1_w[b][:, a, :].bitcast(FP4X4),
                        rhs_scale=w1_sc[:, a, b * PASS : (b + 1) * PASS],
                        start=(a == 0),
                        stop=(a == KP - 1),
                    )
                banks.append(acc)
            return th, at, banks

        def empty(half, slots, by_bank):
            th, at, banks = half
            for group in ([[jl] for jl in range(4)] if by_bank else [range(4)]):
                for jl in group:
                    nc.scalar.activation(th[:, jl, slots, :], banks[jl][:].rearrange("p (q t) -> p t q", t=PACK)[:, slots, :], ACT.Tanh)
                for jl in group:
                    nc.scalar.copy(at[:, jl, slots, :], banks[jl][:].rearrange("p (q t) -> p t q", t=PACK)[:, slots, :])

        def load_page(b, t):
            pg = wide([P, T2], F32, "page%d%d" % (b, t))
            nc.sync.dma_start(pg[:], rows(page0, b, t))
            return pg

        wg = [keep.tile([P, S], F32, name="wg%d" % t, tag="wg%d" % t, align_bytes=64) for t in range(PACK)]

        def load_wg(t):
            for g in (0, 2, 1, 3):
                nc.sync.dma_start(wg[t][32 * g : 32 * g + 32, :], wgs.rearrange("(q t) j -> q t j", t=PACK)[:, t, :])

        def make_h(b, t, h, mx, th, at, hh):
            mt = psum.tile([P, 4, P], F32, name="mt")
            for jl in range(4):
                nc.tensor.transpose(mt[:, jl, :], mx[:, (4 * h + jl) * P : (4 * h + jl + 1) * P], ident[:])
            if (b, t) < (0, 2):
                nc.vector.tensor_tensor(th[:, :, t, :], mt[:], th[:, :, t, :], ALU.mult)
            else:
                turned = mx[:, half_cols(h)].rearrange("p (a b) -> p a b", a=4)
                nc.scalar.copy(turned, mt[:])
                nc.gpsimd.tensor_tensor(th[:, :, t, :], turned, th[:, :, t, :], ALU.mult)
            hb = psum.tile([P, 4, P], F32, name="hb")
            for jl in range(4):
                nc.tensor.matmul(hb[:, jl, :], at[:, jl, t, :], ident[:], start=(jl == 0), stop=False, is_transpose=True)
            for jl in range(4):
                nc.tensor.matmul(hb[:, jl, :], th[:, jl, t, :], ident[:], start=False, stop=(jl == 3), is_transpose=True)
            nc.scalar.activation(hh[:, half_cols(h)], hb[:].rearrange("p a b -> p (a b)"), ACT.Copy, scale=gain_sb[:, b, t : t + 1])
            if (b, t) < (1, 2):
                nc.gpsimd.tensor_tensor(hh[:, half_cols(h)], hh[:, half_cols(h)], wg[t][:, half_cols(h)], ALU.mult)

        def weave(dst, src):
            nc.scalar.copy(dst.rearrange("p (c i) t -> p c t i", i=4), src.rearrange("p t (c i) -> p c t i", i=4))

        def weave_ring(src, name):
            xi = ring.tile([P, HALF * PACK], BF16, name=name, tag="xi", align_bytes=64)[:]
            weave(xi.rearrange("p (c t) -> p c t", t=PACK), src)
            return xi

        def quantise_woven(xi, codes, scales):
            nc.vector.quantize_mx(out=codes.bitcast(FP8X4), scales=scales, in_=xi)

        def quantise(src, codes, scales, name):
            quantise_woven(weave_ring(src, name), codes, scales)

        w4_c = [keep.tile([P, N], U32, name="w4c%d" % b, align_bytes=64) for b in range(HP)]
        w4_s = [keep.tile([P, N], U8, name="w4s%d" % b, align_bytes=64) for b in range(HP)]
        x_c = {1: [keep.tile([P, HALF], U32, name="xc1%d" % m, tag="xc1%d" % m, align_bytes=64)[:] for m in range(2)]}
        x_s = [[keep.tile([P, HALF], U8, name="xs%d%d" % (b, m), align_bytes=64) for m in range(2)] for b in range(HP)]

        def do_w4(b):
            raw = wide([P, PACK, N], F32, "w4raw%d" % b)
            nc.sync.dma_start(raw[:], w4[b * PASS : (b + 1) * PASS, :].rearrange("(p t) n -> p t n", t=PACK))
            quantise(raw[:], w4_c[b][:], w4_s[b][:], "w4i%d" % b)

        def fetch(plane, pg, offsets):
            nc.vector.tensor_copy(plane, pg[:].indirect(offsets))

        def floor(plane, b, t):
            nc.vector.tensor_scalar(plane, plane, low_sb[:, b, t : t + 1], None, ALU.max)

        outs = {}

        def load_out(q):
            pg = wide([P, T2], F32, "outp%d" % q)
            nc.sync.dma_start(pg[:], page1[q * P : (q + 1) * P, :])
            outs[q] = pg

        wgo_sb = keep.tile([P, M], F32)
        units = [(b, t) for b in range(HP) for t in range(PACK)]
        n_units = len(units)
        SLOT = 2 * S
        arena = keep.tile([P, 10 * S + S // 2], F32, align_bytes=64)
        arena16 = arena[:].bitcast(BF16)

        def run16(slot, start, width):
            return arena16[:, slot * SLOT + start : slot * SLOT + start + width]

        def planes16(slot, start, width):
            base = slot * SLOT + start + width - SLOT
            return arena16[:, base : base + PACK * SLOT].rearrange("p (t c) -> p t c", t=PACK)[:, :, SLOT - width : SLOT]

        def raw(u):
            return run16(u + 1, 0, M) if u < PACK else run16(u + 1, HALF, HALF)

        def floored(u):
            return run16(u + 2, M, M) if u < PACK else run16(u + 2, 0, HALF)

        def fetch_unit(u):
            fetch(raw(u), pages[units[u]], l_get[:] if u < PACK else half_offsets(l_get, 0))

        def floor_unit(u):
            b, t = units[u]
            nc.vector.tensor_scalar(floored(u), raw(u), low_sb[:, b, t : t + 1], None, ALU.max)

        x_c[0] = {}
        halves = {}
        mixes = {units[0]: load_mix(0, 0)}
        pages = {units[0]: load_page(0, 0)}
        load_wg(0)
        mixes[units[1]] = load_mix(0, 1)
        pages[units[1]] = load_page(0, 1)
        load_wg(1)

        def h_slot(u):
            return arena[:, u * S : (u + 1) * S]

        def h_half(u, h):
            b, t = units[u]
            make_h(b, t, h, mixes[b, t], halves[b, h][0], halves[b, h][1], h_slot(u))

        halves[0, 0] = first_product(0, 0)
        empty(halves[0, 0], slice(0, 1), False)
        h_half(0, 0)
        empty(halves[0, 0], slice(1, PACK), True)
        h_half(1, 0)
        halves[0, 1] = first_product(0, 1)
        empty(halves[0, 1], slice(0, 2), False)
        h_half(0, 1)
        h_half(1, 1)
        empty(halves[0, 1], slice(2, PACK), True)
        woven = {}
        for u, (b, t) in enumerate(units):
            last = u == n_units - 1
            if u == PACK:
                for h in range(2):
                    halves[b, h] = first_product(b, h)
                    empty(halves[b, h], slice(0, PACK), True)
            hh = h_slot(u)
            if u in (2, 3):
                load_wg(t)
            for h in range(2 if u >= 2 else 0):
                h_half(u, h)
            if last:
                for m, tag in ((0, "th2"), (1, "th0")):
                    woven[m] = keep.tile([P, HALF * PACK], BF16, name="xi0%d" % m, tag=tag, align_bytes=64)[:]
                    weave(woven[m].rearrange("p (c t) -> p c t", t=PACK), planes16(2, M + m * HALF, HALF))
            if u > 1 and not last:
                mixes[units[u + 1]] = load_mix(*units[u + 1])
            if u > 1:
                pages[b, t] = load_page(b, t)
            if u == 1:
                nc.sync.dma_start(l_get[:], offs3)
                nc.sync.dma_start(low_sb[:], low.rearrange("(b p t) -> p b t", b=HP, t=PACK))
                mixes[units[2]] = load_mix(*units[2])
            if u == 2:
                load_w1(1)
            if u < 2:
                for h in range(2):
                    nc.vector.tensor_copy(pages[b, t][:].indirect(half_offsets(l_put, h)), hh[:, half_cols(h)])
            elif u < 6:
                nc.vector.tensor_copy(pages[b, t][:].indirect(l_put[:]), hh)
            else:
                nc.vector.tensor_tensor(pages[b, t][:].indirect(l_put[:]), hh, wg[t][:], ALU.mult)
            if u >= 2:
                floor_unit(u - 2)
            if u >= 1:
                fetch_unit(u - 1)
            if u in (3, 4):
                do_w4(u - 3)
            if u == 4:
                nc.sync.dma_start(l_out[:], offs4)
            if u == 5:
                load_out(0)
                load_out(1)
            if u == 6:
                nc.sync.dma_start(wgo_sb[:], wgo)
                with nc.allow_non_contiguous_dma(reason="one target value a partition"):
                    nc.sync.dma_start(target_sb[:], target.rearrange("(q p) -> p q", p=P))
        load_out(2)
        load_out(3)

        fetch_unit(7)
        floor_unit(6)
        floor_unit(7)
        xi10 = run16(9, 768, PACK * HALF)
        weave(xi10.rearrange("p (c t) -> p c t", t=PACK), planes16(6, 0, HALF))
        x_c[0][0] = keep.tile([P, HALF], U32, name="xc00", tag="wg2", align_bytes=64)[:]
        quantise_woven(woven[0], x_c[0][0], x_s[0][0][:])
        x_c[0][1] = keep.tile([P, HALF], U32, name="xc01", tag="wg3", align_bytes=64)[:]
        quantise_woven(woven[1], x_c[0][1], x_s[0][1][:])
        quantise_woven(xi10, x_c[1][0], x_s[1][0][:])
        planes11 = planes16(7, HALF, HALF)
        for t in range(PACK):
            fetch(run16(7 + t, HALF, HALF), pages[1, t], half_offsets(l_get, 1))
        for t in range(PACK):
            floor(run16(7 + t, HALF, HALF), 1, t)

        def second(q, m):
            acc = psum.tile([P, HALF], F32, name="acc", bufs=4)
            for b in range(HP):
                nc.tensor.matmul_mx(
                    out=acc[:],
                    lhsT=w4_c[b][:, q * P : (q + 1) * P].bitcast(FP8X4),
                    lhsT_scale=w4_s[b][:, q * P : (q + 1) * P],
                    rhs=x_c[b][m].bitcast(FP8X4),
                    rhs_scale=x_s[b][m][:],
                    start=(b == 0),
                    stop=(b == HP - 1),
                )
            y = arena[:, q * M + m * HALF : q * M + (m + 1) * HALF]
            nc.scalar.activation(y, acc[:], ACT.Square, bias=target_sb[:, q : q + 1], scale=-1.0)
            if q < 2:
                nc.vector.tensor_tensor(outs[q][:].indirect(half_offsets(l_out, m)), y, wgo_sb[:, half_cols(m)], ALU.mult)
            elif m == 1:
                nc.vector.tensor_tensor(outs[q][:].indirect(l_out[:]), arena[:, q * M : (q + 1) * M], wgo_sb[:], ALU.mult)
            if m == 1:
                nc.sync.dma_start(out[q * P : (q + 1) * P, :], outs[q][:])

        second(0, 0)
        second(1, 0)
        quantise(planes11, x_c[1][1], x_s[1][1][:], "xi11")
        for q, m in ((0, 1), (1, 1), (2, 0), (2, 1), (3, 0), (3, 1)):
            second(q, m)
